import numpy as np
import ml_dtypes


def mxq(x, axis, fmt="e4m3"):
    dtype, down = {"e4m3": (ml_dtypes.float8_e4m3fn, 7), "e5m2": (ml_dtypes.float8_e5m2, 14)}[fmt]
    v = np.moveaxis(np.asarray(x, np.float32).astype(ml_dtypes.bfloat16).astype(np.float64), axis, -1)
    blocks = v.reshape(v.shape[:-1] + (-1, 32))
    amax = np.abs(blocks).max(-1, keepdims=True)
    byte = np.maximum(np.where(amax > 0, np.frexp(amax)[1] - 1 + 127, 0) - down, 1)
    scale = np.exp2(byte - 127.0)
    codes = (blocks / scale).astype(np.float32).astype(dtype).astype(np.float64)
    return np.moveaxis((codes * scale).reshape(v.shape), -1, axis)


WIDE = False


def mx_kscale(k):
    if not WIDE:
        return np.ones(k)
    levels = np.array([10, -10, 5, -5, 0])
    if k % 512:
        return np.exp2(np.random.permutation(np.resize(levels, k // 32))).repeat(32)
    a = np.empty((k // 512, 16))
    for p in range(k // 512):
        a[p, :8] = np.random.permutation(np.resize(levels, 8))
        for g in range(8):
            far = levels[np.abs(levels - a[p, g]) >= 10]
            a[p, g + 8] = far[np.random.randint(len(far))]
    return np.exp2(a.ravel()).repeat(32)


def f64(x):
    return np.asarray(x).astype(np.float64)


def striped(idx):
    return np.tile(idx.reshape(-1, 16).T, (8, 1)).astype(np.uint16)


def unstriped(offs):
    return offs[:16].T.reshape(-1).astype(np.int64)


def relu(v):
    return np.maximum(v, 0.0)


K, T, E, C, H, N = 512, 768, 6, 256, 512, 512


def by_expert(wq, xq):
    return np.concatenate([wq[e].T @ xq[:, e * C:(e + 1) * C] for e in range(E)], axis=1)


def setup_inputs():
    n = np.random.standard_normal
    s = mx_kscale(K)[:, None]
    u = mx_kscale(H)
    first = np.random.permutation(np.repeat(np.arange(E), T // E))
    second = (first + 1 + np.random.permutation(np.repeat(np.arange(E - 1), -(-T // (E - 1)))[:T])) % E
    while np.bincount(second, minlength=E).max() != T // E:
        load = np.bincount(second, minlength=E); hi, lo = int(load.argmax()), int(load.argmin())
        t = np.flatnonzero((second == hi) & (first != lo))[0]; second[t] = lo
    slot_token = np.empty(E * C, np.int64); pos = np.empty((2, T), np.int64); fill = np.zeros(E, np.int64)
    place = np.stack([np.random.permutation(C) for _ in range(E)])
    for r, deal in enumerate((first, second)):
        for t in np.random.permutation(T):
            e = deal[t]; j = e * C + place[e, fill[e]]; fill[e] += 1; slot_token[j] = t; pos[r, t] = j
    g = np.random.uniform(0.2, 0.8, T)
    return {
        "xT": (n((K, T)) * s).astype(np.float32),
        "w1": (n((E, K, H)) / np.sqrt(K) / s[None] * u[None, None, :]).astype(np.float32),
        "w2": (n((E, H, N)) / np.sqrt(H) / u[None, :, None]).astype(np.float32),
        "gate": np.stack([np.tile(g, (N, 1)), np.tile(1.0 - g, (N, 1))]).astype(np.float32),
        "offs": striped(slot_token),
        "pos1": striped(pos[0]),
        "pos2": striped(pos[1]),
    }


def reference(xT, w1, w2, gate, offs, pos1, pos2):
    idx = unstriped(offs)
    xq = mxq(f64(xT)[:, idx], 0, "e4m3")
    h = relu(by_expert(mxq(f64(w1), 1, "e4m3"), xq))
    y = by_expert(mxq(f64(w2), 1, "e4m3"), mxq(h, 0, "e4m3"))
    return f64(gate[0]) * y[:, unstriped(pos1)] + f64(gate[1]) * y[:, unstriped(pos2)]

@@ -1,0 +1,224 @@
+from contextlib import ExitStack
+
+import concourse.mybir as mybir
+
+K, T, E, C, H, N = 512, 768, 6, 256, 512, 512
+SLOTS = E * C
+FLOPS = 2 * SLOTS * (K * H + H * N)
+
+F32 = mybir.dt.float32
+BF16 = mybir.dt.bfloat16
+U32 = mybir.dt.uint32
+U16 = mybir.dt.uint16
+U8 = mybir.dt.uint8
+FP8X4 = mybir.dt.float8_e4m3fn_x4
+MULT = mybir.AluOpType.mult
+ADD = mybir.AluOpType.add
+RELU = mybir.ActivationFunctionType.Relu
+
+P = 128
+PACK = 4
+NB = N // P
+
+W1_ENGINES = ("SS", "SS", "SV", "VV", "VS", "VV")
+W2_ENGINES = ("VSS", "VVS", "SVS", "SSS")
+H_ENGINES = "VSSSSSSSSSSV"
+Y_ENGINES = "SSSSSSSSSSSS"
+X_ENGINES = "VSV"
+
+
+def tile_routed_moe_kernel(tc, xT, w1, w2, gate, offs, pos1, pos2, out):
+    nc = tc.nc
+
+    def copy(engine, dst, src):
+        if engine == "S":
+            nc.scalar.copy(dst, src)
+        elif engine == "G":
+            nc.gpsimd.tensor_copy(dst, src)
+        else:
+            nc.vector.tensor_copy(dst, src)
+
+    with ExitStack() as ctx:
+        lists = ctx.enter_context(tc.tile_pool(name="lists", bufs=1))
+        offs_t = lists.tile([P, SLOTS // 16], U16, name="offs_t")
+        pos1_t = lists.tile([P, T // 16], U16, name="pos1_t")
+        pos2_t = lists.tile([P, T // 16], U16, name="pos2_t")
+
+        keep = ctx.enter_context(tc.tile_pool(name="keep", bufs=1))
+        w1g_pool = ctx.enter_context(tc.tile_pool(name="w1g_pool", bufs=2))
+        stage = ctx.enter_context(tc.tile_pool(name="stage", bufs=3))
+        y_pool = ctx.enter_context(tc.tile_pool(name="y_pool", bufs=2))
+        work = ctx.enter_context(tc.tile_pool(name="work", bufs=2))
+        psum_h = ctx.enter_context(tc.psum_pool(name="psum_h", bufs=4))
+        psum_y = ctx.enter_context(tc.psum_pool(name="psum_y", bufs=4))
+
+        x_cuts = ((0, 512), (512, 768))
+        x_view = xT.rearrange("(p j) t -> p j t", j=PACK)
+        x_raw = []
+        for i, (a, b) in enumerate(x_cuts):
+            t = keep.tile([P, PACK, b - a], F32, name=f"x_raw{i}")
+            nc.sync.dma_start(out=t[:], in_=x_view[:, :, a:b])
+            x_raw.append(t)
+            if i == 0:
+                nc.sync.dma_start(offs_t[:], offs)
+        w1_raw = []
+        for e in range(E):
+            t = keep.tile([P, PACK, H], F32, name=f"w1_raw{e}")
+            nc.sync.dma_start(out=t[:], in_=w1[e].rearrange("(p j) h -> p j h", j=PACK))
+            w1_raw.append(t)
+        nc.sync.dma_start(pos1_t[:], pos1)
+        nc.sync.dma_start(pos2_t[:], pos2)
+        w2_raw, gates = {}, {}
+        for b in range(NB):
+            cols = slice(b * P, (b + 1) * P)
+            for q in range(E // 2):
+                t = keep.tile([P, 2, PACK, P], F32, name=f"w2_raw{b}_{q}")
+                for r in range(2):
+                    nc.sync.dma_start(out=t[:, r, :, :], in_=w2[2 * q + r].rearrange("(p j) n -> p j n", j=PACK)[:, :, cols])
+                w2_raw[b, q] = t
+            for g in range(2):
+                t = keep.tile([P, T], F32, name=f"gate{b}_{g}")
+                nc.sync.dma_start(out=t[:], in_=gate[g, cols, :])
+                gates[b, g] = t
+
+        xq = keep.tile([P, T], U32, name="xq", align_bytes=64)
+        xs = keep.tile([P, T], U8, name="xs", align_bytes=64)
+        nc.gpsimd.memset(xs[:], 0)
+        for i, (a, b) in enumerate(x_cuts):
+            t = keep.tile([P, b - a, PACK], BF16, name=f"x_grp{i}", align_bytes=64)
+            for c in range(a, b, 256):
+                part = slice(c - a, c - a + 256)
+                copy(X_ENGINES[c // 256], t[:, part, :], x_raw[i][:, :, part].rearrange("p j t -> p t j"))
+            nc.vector.quantize_mx(out=xq[:, a:b].bitcast(FP8X4), scales=xs[:, a:b], in_=t[:].rearrange("p t j -> p (t j)"))
+        xq_slots = keep.tile([P, SLOTS], U32, name="xq_slots", align_bytes=64)
+        xs_slots = keep.tile([P, SLOTS], U8, name="xs_slots", align_bytes=64)
+
+        def gather(a, b):
+            o = slice(a // 16, b // 16)
+            nc.vector.tensor_copy(xq_slots[:, a:b], xq[:].indirect(offs_t[:, o]))
+            nc.vector.tensor_copy(xs_slots[:, a:b], xs[:].indirect(offs_t[:, o]))
+
+        w1_codes, w1_scales, h_codes, h_scales = [], [], [], []
+
+        def prepare_w1(e):
+            grp = w1g_pool.tile([P, H, PACK], BF16, name="w1_grp", align_bytes=64)
+            half = H // PACK // 2
+            for i in range(2):
+                m = slice(i * half, (i + 1) * half)
+                copy(
+                    W1_ENGINES[e][i],
+                    grp[:].rearrange("p (t m) j -> p m t j", t=PACK)[:, m, :, :],
+                    w1_raw[e][:].rearrange("p j (m t) -> p m t j", t=PACK)[:, m, :, :],
+                )
+            codes = keep.tile([P, H], U32, name=f"w1_codes{e}", align_bytes=64)
+            scales = keep.tile([P, H], U8, name=f"w1_scales{e}", align_bytes=64)
+            nc.vector.quantize_mx(out=codes[:].bitcast(FP8X4), scales=scales[:], in_=grp[:].rearrange("p h j -> p (h j)"))
+            w1_codes.append(codes)
+            w1_scales.append(scales)
+
+        h_grp = {}
+
+        def layer1(e):
+            grp = stage.tile([P, C, PACK], BF16, name="h_grp", align_bytes=64)
+            for u in range(2):
+                bank = psum_h.tile([P, PACK, P], F32, name="h_bank")
+                slots = slice(e * C + u * P, e * C + (u + 1) * P)
+                for t in range(PACK):
+                    cols = slice(t * P, (t + 1) * P)
+                    nc.tensor.matmul_mx(
+                        out=bank[:, t, :],
+                        lhsT=w1_codes[e][:, cols].bitcast(FP8X4),
+                        lhsT_scale=w1_scales[e][:, cols],
+                        rhs=xq_slots[:, slots].bitcast(FP8X4),
+                        rhs_scale=xs_slots[:, slots],
+                        start=True,
+                        stop=True,
+                    )
+                dst, src = grp[:, u * P : (u + 1) * P, :], bank[:].rearrange("p t s -> p s t")
+                if H_ENGINES[2 * e + u] == "S":
+                    nc.scalar.activation(dst, src, RELU)
+                else:
+                    nc.vector.tensor_relu(dst, src)
+            h_grp[e] = grp
+
+        def quantize_h(e):
+            codes = keep.tile([P, C], U32, name=f"h_codes{e}", align_bytes=64)
+            scales = keep.tile([P, C], U8, name=f"h_scales{e}", align_bytes=64)
+            nc.vector.quantize_mx(out=codes[:].bitcast(FP8X4), scales=scales[:], in_=h_grp[e][:].rearrange("p s j -> p (s j)"))
+            h_codes.append(codes)
+            h_scales.append(scales)
+
+        w2_codes, w2_scales = {}, {}
+
+        def prepare_w2(b, q):
+            grp = stage.tile([P, 2, P, PACK], BF16, name="w2_grp", align_bytes=64)
+            copy(W2_ENGINES[b][q], grp[:], w2_raw[b, q][:].rearrange("p r j n -> p r n j"))
+            codes = stage.tile([P, 2 * P], U32, name="w2_codes", align_bytes=64)
+            scales = stage.tile([P, 2 * P], U8, name="w2_scales", align_bytes=64)
+            nc.vector.quantize_mx(out=codes[:].bitcast(FP8X4), scales=scales[:], in_=grp[:].rearrange("p r n j -> p (r n j)"))
+            w2_codes[b, q], w2_scales[b, q] = codes, scales
+
+        y_tiles = {}
+
+        def layer2(b, q):
+            if q == 0:
+                y_tiles[b] = y_pool.tile([P, SLOTS], F32, name="y")
+            bank = psum_y.tile([P, 2 * C], F32, name="y_bank")
+            for r in range(2):
+                cols = slice(r * P, (r + 1) * P)
+                nc.tensor.matmul_mx(
+                    out=bank[:, r * C : (r + 1) * C],
+                    lhsT=w2_codes[b, q][:, cols].bitcast(FP8X4),
+                    lhsT_scale=w2_scales[b, q][:, cols],
+                    rhs=h_codes[2 * q + r][:].bitcast(FP8X4),
+                    rhs_scale=h_scales[2 * q + r][:],
+                    start=True,
+                    stop=True,
+                )
+            copy(Y_ENGINES[b * 3 + q], y_tiles[b][:, q * 2 * C : (q + 1) * 2 * C], bank[:])
+
+        def combine(b):
+            first = work.tile([P, T], F32, name="first")
+            second = work.tile([P, T], F32, name="second")
+            cuts = ((0, 384), (384, 768)) if b == NB - 1 else ((0, T),)
+            y = y_tiles[b]
+            for a, z in cuts:
+                o = slice(a // 16, z // 16)
+                nc.vector.tensor_tensor(first[:, a:z], y[:].indirect(pos1_t[:, o]), gates[b, 0][:, a:z], MULT)
+                nc.vector.tensor_tensor(second[:, a:z], y[:].indirect(pos2_t[:, o]), gates[b, 1][:, a:z], MULT)
+                nc.vector.tensor_tensor(first[:, a:z], first[:, a:z], second[:, a:z], ADD)
+                nc.sync.dma_start(out=out[b * P : (b + 1) * P, a:z], in_=first[:, a:z])
+
+        gather(0, 512)
+        prepare_w1(0)
+        prepare_w1(1)
+        layer1(0)
+        gather(512, 1024)
+        layer1(1)
+        prepare_w1(2)
+        quantize_h(0)
+        layer1(2)
+        prepare_w1(3)
+        quantize_h(1)
+        gather(1024, 1536)
+        layer1(3)
+        prepare_w1(4)
+        quantize_h(2)
+        layer1(4)
+        prepare_w1(5)
+        quantize_h(3)
+        layer1(5)
+        quantize_h(4)
+        prepare_w2(0, 0)
+        layer2(0, 0)
+        prepare_w2(0, 1)
+        quantize_h(5)
+        layer2(0, 1)
+        prepare_w2(0, 2)
+        layer2(0, 2)
+        for b in range(NB):
+            combine(b)
+            if b + 1 < NB:
+                for q in range(E // 2):
+                    prepare_w2(b + 1, q)
+                    layer2(b + 1, q)

@@ -20,9 +20,9 @@ P = 128
 PACK = 4
 NB = N // P
 
-W1_ENGINES = ("SS", "SS", "SV", "VV", "VS", "VV")
-W2_ENGINES = ("VSS", "VVS", "SVS", "SSS")
-H_ENGINES = "VSSSSSSSSSSV"
+W1_ENGINES = ("S", "S", "SV", "V", "SV", "V")
+W2_ENGINES = (("S", "V", "S"), ("VS", "S", "S"))
+H_ENGINES = "SSSSSSSSSSSS"
 Y_ENGINES = "SSSSSSSSSSSS"
 X_ENGINES = "VSV"
 
@@ -34,7 +34,7 @@ def tile_routed_moe_kernel(tc, xT, w1, w2, gate, offs, pos1, pos2, out):
         if engine == "S":
             nc.scalar.copy(dst, src)
         elif engine == "G":
-            nc.gpsimd.tensor_copy(dst, src)
+            nc.gpsimd.tensor_scalar(dst, src, 1.0, 0.0, MULT, ADD)
         else:
             nc.vector.tensor_copy(dst, src)
 
@@ -45,10 +45,13 @@ def tile_routed_moe_kernel(tc, xT, w1, w2, gate, offs, pos1, pos2, out):
         pos2_t = lists.tile([P, T // 16], U16, name="pos2_t")
 
         keep = ctx.enter_context(tc.tile_pool(name="keep", bufs=1))
-        w1g_pool = ctx.enter_context(tc.tile_pool(name="w1g_pool", bufs=2))
-        stage = ctx.enter_context(tc.tile_pool(name="stage", bufs=3))
+        w1g_pool = ctx.enter_context(tc.tile_pool(name="w1g_pool", bufs=3))
+        w2_pool = ctx.enter_context(tc.tile_pool(name="w2_pool", bufs=4))
+        h_pool = ctx.enter_context(tc.tile_pool(name="h_pool", bufs=3))
+        slot_pool = ctx.enter_context(tc.tile_pool(name="slot_pool", bufs=2))
         y_pool = ctx.enter_context(tc.tile_pool(name="y_pool", bufs=2))
         work = ctx.enter_context(tc.tile_pool(name="work", bufs=2))
+        raw_pool = ctx.enter_context(tc.tile_pool(name="raw_pool", bufs=9))
         psum_h = ctx.enter_context(tc.psum_pool(name="psum_h", bufs=4))
         psum_y = ctx.enter_context(tc.psum_pool(name="psum_y", bufs=4))
 
@@ -63,23 +66,30 @@ def tile_routed_moe_kernel(tc, xT, w1, w2, gate, offs, pos1, pos2, out):
                 nc.sync.dma_start(offs_t[:], offs)
         w1_raw = []
         for e in range(E):
-            t = keep.tile([P, PACK, H], F32, name=f"w1_raw{e}")
+            t = raw_pool.tile([P, PACK, H], F32, name="raw")
             nc.sync.dma_start(out=t[:], in_=w1[e].rearrange("(p j) h -> p j h", j=PACK))
             w1_raw.append(t)
         nc.sync.dma_start(pos1_t[:], pos1)
         nc.sync.dma_start(pos2_t[:], pos2)
         w2_raw, gates = {}, {}
-        for b in range(NB):
-            cols = slice(b * P, (b + 1) * P)
+
+        def load_w2(half):
+            cols = slice(half * 2 * P, (half + 1) * 2 * P)
             for q in range(E // 2):
-                t = keep.tile([P, 2, PACK, P], F32, name=f"w2_raw{b}_{q}")
+                t = raw_pool.tile([P, PACK, 4 * P], F32, name="raw")
                 for r in range(2):
-                    nc.sync.dma_start(out=t[:, r, :, :], in_=w2[2 * q + r].rearrange("(p j) n -> p j n", j=PACK)[:, :, cols])
-                w2_raw[b, q] = t
-            for g in range(2):
-                t = keep.tile([P, T], F32, name=f"gate{b}_{g}")
-                nc.sync.dma_start(out=t[:], in_=gate[g, cols, :])
-                gates[b, g] = t
+                    nc.sync.dma_start(
+                        out=t[:, :, r * 2 * P : (r + 1) * 2 * P],
+                        in_=w2[2 * q + r].rearrange("(p j) n -> p j n", j=PACK)[:, :, cols],
+                    )
+                w2_raw[half, q] = t
+            for b in (2 * half, 2 * half + 1):
+                for g in range(2):
+                    t = keep.tile([P, T], F32, name=f"gate{b}_{g}")
+                    nc.sync.dma_start(out=t[:], in_=gate[g, b * P : (b + 1) * P, :])
+                    gates[b, g] = t
+
+        load_w2(0)
 
         xq = keep.tile([P, T], U32, name="xq", align_bytes=64)
         xs = keep.tile([P, T], U8, name="xs", align_bytes=64)
@@ -88,27 +98,35 @@ def tile_routed_moe_kernel(tc, xT, w1, w2, gate, offs, pos1, pos2, out):
             t = keep.tile([P, b - a, PACK], BF16, name=f"x_grp{i}", align_bytes=64)
             for c in range(a, b, 256):
                 part = slice(c - a, c - a + 256)
-                copy(X_ENGINES[c // 256], t[:, part, :], x_raw[i][:, :, part].rearrange("p j t -> p t j"))
+                copy(
+                    X_ENGINES[c // 256],
+                    t[:, part, :].rearrange("p (c i) j -> p c j i", i=4),
+                    x_raw[i][:, :, part].rearrange("p j (c i) -> p c j i", i=4),
+                )
             nc.vector.quantize_mx(out=xq[:, a:b].bitcast(FP8X4), scales=xs[:, a:b], in_=t[:].rearrange("p t j -> p (t j)"))
-        xq_slots = keep.tile([P, SLOTS], U32, name="xq_slots", align_bytes=64)
-        xs_slots = keep.tile([P, SLOTS], U8, name="xs_slots", align_bytes=64)
+        xq_slots, xs_slots = [], []
 
-        def gather(a, b):
-            o = slice(a // 16, b // 16)
-            nc.vector.tensor_copy(xq_slots[:, a:b], xq[:].indirect(offs_t[:, o]))
-            nc.vector.tensor_copy(xs_slots[:, a:b], xs[:].indirect(offs_t[:, o]))
+        def gather(q):
+            o = slice(q * 2 * C // 16, (q + 1) * 2 * C // 16)
+            words = slot_pool.tile([P, 2 * C], U32, name="words", align_bytes=64)
+            scales = slot_pool.tile([P, 2 * C], U8, name="scales", align_bytes=64)
+            nc.vector.tensor_copy(words[:], xq[:].indirect(offs_t[:, o]))
+            nc.vector.tensor_copy(scales[:], xs[:].indirect(offs_t[:, o]))
+            xq_slots.append(words)
+            xs_slots.append(scales)
 
         w1_codes, w1_scales, h_codes, h_scales = [], [], [], []
 
         def prepare_w1(e):
             grp = w1g_pool.tile([P, H, PACK], BF16, name="w1_grp", align_bytes=64)
-            half = H // PACK // 2
-            for i in range(2):
-                m = slice(i * half, (i + 1) * half)
+            parts = W1_ENGINES[e]
+            size = P // len(parts)
+            for i in range(len(parts)):
+                m = slice(i * size, (i + 1) * size)
                 copy(
-                    W1_ENGINES[e][i],
-                    grp[:].rearrange("p (t m) j -> p m t j", t=PACK)[:, m, :, :],
-                    w1_raw[e][:].rearrange("p j (m t) -> p m t j", t=PACK)[:, m, :, :],
+                    parts[i],
+                    grp[:].rearrange("p (t m) j -> p m j t", t=PACK)[:, m, :, :],
+                    w1_raw[e][:].rearrange("p j (m t) -> p m j t", t=PACK)[:, m, :, :],
                 )
             codes = keep.tile([P, H], U32, name=f"w1_codes{e}", align_bytes=64)
             scales = keep.tile([P, H], U8, name=f"w1_scales{e}", align_bytes=64)
@@ -119,44 +137,54 @@ def tile_routed_moe_kernel(tc, xT, w1, w2, gate, offs, pos1, pos2, out):
         h_grp = {}
 
         def layer1(e):
-            grp = stage.tile([P, C, PACK], BF16, name="h_grp", align_bytes=64)
+            if e % 2 == 0:
+                h_grp[e // 2] = h_pool.tile([P, 2 * C, PACK], BF16, name="h_grp", align_bytes=64)
+            grp = h_grp[e // 2]
+            base = e % 2 * C
             for u in range(2):
                 bank = psum_h.tile([P, PACK, P], F32, name="h_bank")
-                slots = slice(e * C + u * P, e * C + (u + 1) * P)
+                slots = slice(base + u * P, base + (u + 1) * P)
                 for t in range(PACK):
                     cols = slice(t * P, (t + 1) * P)
                     nc.tensor.matmul_mx(
                         out=bank[:, t, :],
                         lhsT=w1_codes[e][:, cols].bitcast(FP8X4),
                         lhsT_scale=w1_scales[e][:, cols],
-                        rhs=xq_slots[:, slots].bitcast(FP8X4),
-                        rhs_scale=xs_slots[:, slots],
+                        rhs=xq_slots[e // 2][:, slots].bitcast(FP8X4),
+                        rhs_scale=xs_slots[e // 2][:, slots],
                         start=True,
                         stop=True,
                     )
-                dst, src = grp[:, u * P : (u + 1) * P, :], bank[:].rearrange("p t s -> p s t")
+                dst, src = grp[:, base + u * P : base + (u + 1) * P, :], bank[:].rearrange("p t s -> p s t")
                 if H_ENGINES[2 * e + u] == "S":
                     nc.scalar.activation(dst, src, RELU)
                 else:
                     nc.vector.tensor_relu(dst, src)
-            h_grp[e] = grp
 
-        def quantize_h(e):
-            codes = keep.tile([P, C], U32, name=f"h_codes{e}", align_bytes=64)
-            scales = keep.tile([P, C], U8, name=f"h_scales{e}", align_bytes=64)
-            nc.vector.quantize_mx(out=codes[:].bitcast(FP8X4), scales=scales[:], in_=h_grp[e][:].rearrange("p s j -> p (s j)"))
+        def quantize_h(q):
+            codes = keep.tile([P, 2 * C], U32, name=f"h_codes{q}", align_bytes=64)
+            scales = keep.tile([P, 2 * C], U8, name=f"h_scales{q}", align_bytes=64)
+            nc.vector.quantize_mx(out=codes[:].bitcast(FP8X4), scales=scales[:], in_=h_grp[q][:].rearrange("p s j -> p (s j)"))
             h_codes.append(codes)
             h_scales.append(scales)
 
         w2_codes, w2_scales = {}, {}
 
-        def prepare_w2(b, q):
-            grp = stage.tile([P, 2, P, PACK], BF16, name="w2_grp", align_bytes=64)
-            copy(W2_ENGINES[b][q], grp[:], w2_raw[b, q][:].rearrange("p r j n -> p r n j"))
-            codes = stage.tile([P, 2 * P], U32, name="w2_codes", align_bytes=64)
-            scales = stage.tile([P, 2 * P], U8, name="w2_scales", align_bytes=64)
-            nc.vector.quantize_mx(out=codes[:].bitcast(FP8X4), scales=scales[:], in_=grp[:].rearrange("p r n j -> p (r n j)"))
-            w2_codes[b, q], w2_scales[b, q] = codes, scales
+        def prepare_w2(half, q):
+            grp = h_pool.tile([P, 4 * P, PACK], BF16, name="w2_grp", align_bytes=64)
+            parts = W2_ENGINES[half][q]
+            size = 4 * P // len(parts)
+            for i in range(len(parts)):
+                n = slice(i * size, (i + 1) * size)
+                copy(
+                    parts[i],
+                    grp[:, n, :].rearrange("p (c i) j -> p c j i", i=4),
+                    w2_raw[half, q][:, :, n].rearrange("p j (c i) -> p c j i", i=4),
+                )
+            codes = w2_pool.tile([P, 4 * P], U32, name="w2_codes", align_bytes=64)
+            scales = w2_pool.tile([P, 4 * P], U8, name="w2_scales", align_bytes=64)
+            nc.vector.quantize_mx(out=codes[:].bitcast(FP8X4), scales=scales[:], in_=grp[:].rearrange("p n j -> p (n j)"))
+            w2_codes[half, q], w2_scales[half, q] = codes, scales
 
         y_tiles = {}
 
@@ -165,13 +193,13 @@ def tile_routed_moe_kernel(tc, xT, w1, w2, gate, offs, pos1, pos2, out):
                 y_tiles[b] = y_pool.tile([P, SLOTS], F32, name="y")
             bank = psum_y.tile([P, 2 * C], F32, name="y_bank")
             for r in range(2):
-                cols = slice(r * P, (r + 1) * P)
+                cols = slice((2 * r + b % 2) * P, (2 * r + b % 2 + 1) * P)
                 nc.tensor.matmul_mx(
                     out=bank[:, r * C : (r + 1) * C],
-                    lhsT=w2_codes[b, q][:, cols].bitcast(FP8X4),
-                    lhsT_scale=w2_scales[b, q][:, cols],
-                    rhs=h_codes[2 * q + r][:].bitcast(FP8X4),
-                    rhs_scale=h_scales[2 * q + r][:],
+                    lhsT=w2_codes[b // 2, q][:, cols].bitcast(FP8X4),
+                    lhsT_scale=w2_scales[b // 2, q][:, cols],
+                    rhs=h_codes[q][:, r * C : (r + 1) * C].bitcast(FP8X4),
+                    rhs_scale=h_scales[q][:, r * C : (r + 1) * C],
                     start=True,
                     stop=True,
                 )
@@ -189,36 +217,42 @@ def tile_routed_moe_kernel(tc, xT, w1, w2, gate, offs, pos1, pos2, out):
                 nc.vector.tensor_tensor(first[:, a:z], first[:, a:z], second[:, a:z], ADD)
                 nc.sync.dma_start(out=out[b * P : (b + 1) * P, a:z], in_=first[:, a:z])
 
-        gather(0, 512)
+        gather(0)
         prepare_w1(0)
         prepare_w1(1)
         layer1(0)
-        gather(512, 1024)
+        gather(1)
         layer1(1)
         prepare_w1(2)
         quantize_h(0)
         layer1(2)
         prepare_w1(3)
-        quantize_h(1)
-        gather(1024, 1536)
+        gather(2)
         layer1(3)
         prepare_w1(4)
-        quantize_h(2)
+        quantize_h(1)
         layer1(4)
         prepare_w1(5)
-        quantize_h(3)
         layer1(5)
-        quantize_h(4)
+        load_w2(1)
         prepare_w2(0, 0)
+        quantize_h(2)
         layer2(0, 0)
         prepare_w2(0, 1)
-        quantize_h(5)
         layer2(0, 1)
         prepare_w2(0, 2)
         layer2(0, 2)
-        for b in range(NB):
-            combine(b)
-            if b + 1 < NB:
-                for q in range(E // 2):
-                    prepare_w2(b + 1, q)
-                    layer2(b + 1, q)
+        for q in range(E // 2):
+            layer2(1, q)
+        combine(0)
+        prepare_w2(1, 0)
+        layer2(2, 0)
+        prepare_w2(1, 1)
+        layer2(2, 1)
+        combine(1)
+        prepare_w2(1, 2)
+        layer2(2, 2)
+        for q in range(E // 2):
+            layer2(3, q)
+        combine(2)
+        combine(3)

@@ -1,6 +1,7 @@
 from contextlib import ExitStack
 
 import concourse.mybir as mybir
+from concourse.masks import make_identity
 
 K, T, E, C, H, N = 512, 768, 6, 256, 512, 512
 SLOTS = E * C
@@ -19,12 +20,14 @@ RELU = mybir.ActivationFunctionType.Relu
 P = 128
 PACK = 4
 NB = N // P
+PAIR = 2 * C
 
-W1_ENGINES = ("S", "S", "SV", "V", "SV", "V")
-W2_ENGINES = (("S", "V", "S"), ("VS", "S", "S"))
-H_ENGINES = "SSSSSSSSSSSS"
-Y_ENGINES = "SSSSSSSSSSSS"
+X_CUTS = ((0, 512), (512, 768))
 X_ENGINES = "VSV"
+W1_ENGINES = ("S", "S", "S", "S", "VS", "VS")
+H_ENGINES = "SSSSSSVSVSVS"
+ALL = tuple(range(NB))
+W2_GROUPS = (((0,), ALL), ((1,), ALL), ((2,), ALL), ((3,), ALL), ((4, 5), (0, 1)), ((4, 5), (2, 3)))
 
 
 def tile_routed_moe_kernel(tc, xT, w1, w2, gate, offs, pos1, pos2, out):
@@ -33,10 +36,11 @@ def tile_routed_moe_kernel(tc, xT, w1, w2, gate, offs, pos1, pos2, out):
     def copy(engine, dst, src):
         if engine == "S":
             nc.scalar.copy(dst, src)
-        elif engine == "G":
-            nc.gpsimd.tensor_scalar(dst, src, 1.0, 0.0, MULT, ADD)
         else:
             nc.vector.tensor_copy(dst, src)
+
+    def quantize(codes, scales, grouped):
+        nc.vector.quantize_mx(out=codes.bitcast(FP8X4), scales=scales, in_=grouped[:].rearrange("p c j -> p (c j)"))
 
     with ExitStack() as ctx:
         lists = ctx.enter_context(tc.tile_pool(name="lists", bufs=1))
@@ -45,214 +49,226 @@ def tile_routed_moe_kernel(tc, xT, w1, w2, gate, offs, pos1, pos2, out):
         pos2_t = lists.tile([P, T // 16], U16, name="pos2_t")
 
         keep = ctx.enter_context(tc.tile_pool(name="keep", bufs=1))
-        w1g_pool = ctx.enter_context(tc.tile_pool(name="w1g_pool", bufs=3))
-        w2_pool = ctx.enter_context(tc.tile_pool(name="w2_pool", bufs=4))
-        h_pool = ctx.enter_context(tc.tile_pool(name="h_pool", bufs=3))
-        slot_pool = ctx.enter_context(tc.tile_pool(name="slot_pool", bufs=2))
-        y_pool = ctx.enter_context(tc.tile_pool(name="y_pool", bufs=2))
-        work = ctx.enter_context(tc.tile_pool(name="work", bufs=2))
         raw_pool = ctx.enter_context(tc.tile_pool(name="raw_pool", bufs=9))
-        psum_h = ctx.enter_context(tc.psum_pool(name="psum_h", bufs=4))
-        psum_y = ctx.enter_context(tc.psum_pool(name="psum_y", bufs=4))
+        grouped_pool = ctx.enter_context(tc.tile_pool(name="grouped_pool", bufs=3))
+        codes_pool = ctx.enter_context(tc.tile_pool(name="codes_pool", bufs=3))
+        slot_pool = ctx.enter_context(tc.tile_pool(name="slot_pool", bufs=2))
+        y_pool = ctx.enter_context(tc.tile_pool(name="y_pool", bufs=NB))
+        product_pool = ctx.enter_context(tc.tile_pool(name="product_pool", bufs=3))
+        result_pool = ctx.enter_context(tc.tile_pool(name="result_pool", bufs=3))
+        psum_h = ctx.enter_context(tc.psum_pool(name="psum_h", bufs=3))
+        psum_y = ctx.enter_context(tc.psum_pool(name="psum_y", bufs=3))
+        psum_sum = ctx.enter_context(tc.psum_pool(name="psum_sum", bufs=2))
 
-        x_cuts = ((0, 512), (512, 768))
-        x_view = xT.rearrange("(p j) t -> p j t", j=PACK)
-        x_raw = []
-        for i, (a, b) in enumerate(x_cuts):
-            t = keep.tile([P, PACK, b - a], F32, name=f"x_raw{i}")
-            nc.sync.dma_start(out=t[:], in_=x_view[:, :, a:b])
-            x_raw.append(t)
-            if i == 0:
-                nc.sync.dma_start(offs_t[:], offs)
-        w1_raw = []
-        for e in range(E):
-            t = raw_pool.tile([P, PACK, H], F32, name="raw")
-            nc.sync.dma_start(out=t[:], in_=w1[e].rearrange("(p j) h -> p j h", j=PACK))
-            w1_raw.append(t)
+        x_raw, w1_raw, w2_raw, gates = [], [], [], {}
+
+        def load_x(i):
+            a, z = X_CUTS[i]
+            raw = keep.tile([P, PACK, z - a], F32, name=f"x_raw{i}")
+            nc.sync.dma_start(out=raw[:], in_=xT.rearrange("(p j) t -> p j t", j=PACK)[:, :, a:z])
+            x_raw.append(raw)
+
+        def load_w1(e):
+            raw = raw_pool.tile([P, PACK, H], F32, name="raw")
+            nc.sync.dma_start(out=raw[:], in_=w1[e].rearrange("(p j) i -> p j i", j=PACK))
+            w1_raw.append(raw)
+
+        def load_w2(g):
+            experts, blocks = W2_GROUPS[g]
+            width = len(blocks) * P
+            cols = slice(blocks[0] * P, blocks[0] * P + width)
+            raw = raw_pool.tile([P, PACK, len(experts) * width], F32, name="raw")
+            for r, e in enumerate(experts):
+                nc.sync.dma_start(
+                    out=raw[:, :, r * width : (r + 1) * width],
+                    in_=w2[e].rearrange("(p j) n -> p j n", j=PACK)[:, :, cols],
+                )
+            w2_raw.append(raw)
+
+        def load_gates(b):
+            for r in range(2):
+                gates[b, r] = keep.tile([P, T], F32, name=f"gate{b}_{r}")
+                nc.sync.dma_start(out=gates[b, r][:], in_=gate[r, b * P : (b + 1) * P, :])
+
+        load_x(0)
+        nc.sync.dma_start(offs_t[:], offs)
+        load_x(1)
+        load_w1(0)
+        load_w1(1)
+        load_w2(0)
+        load_w2(1)
         nc.sync.dma_start(pos1_t[:], pos1)
         nc.sync.dma_start(pos2_t[:], pos2)
-        w2_raw, gates = {}, {}
+        load_w1(2)
+        load_w1(3)
+        load_w2(2)
+        load_w2(3)
+        load_w1(4)
 
-        def load_w2(half):
-            cols = slice(half * 2 * P, (half + 1) * 2 * P)
-            for q in range(E // 2):
-                t = raw_pool.tile([P, PACK, 4 * P], F32, name="raw")
-                for r in range(2):
-                    nc.sync.dma_start(
-                        out=t[:, :, r * 2 * P : (r + 1) * 2 * P],
-                        in_=w2[2 * q + r].rearrange("(p j) n -> p j n", j=PACK)[:, :, cols],
-                    )
-                w2_raw[half, q] = t
-            for b in (2 * half, 2 * half + 1):
-                for g in range(2):
-                    t = keep.tile([P, T], F32, name=f"gate{b}_{g}")
-                    nc.sync.dma_start(out=t[:], in_=gate[g, b * P : (b + 1) * P, :])
-                    gates[b, g] = t
+        identity = keep.tile([P, P], F32, name="identity")
+        x_codes = keep.tile([P, T], U32, name="x_codes", align_bytes=64)
+        x_scales = keep.tile([P, T], U8, name="x_scales", align_bytes=64)
+        nc.gpsimd.memset(x_scales[:], 0)
+        make_identity(nc, identity[:])
 
-        load_w2(0)
-
-        xq = keep.tile([P, T], U32, name="xq", align_bytes=64)
-        xs = keep.tile([P, T], U8, name="xs", align_bytes=64)
-        nc.gpsimd.memset(xs[:], 0)
-        for i, (a, b) in enumerate(x_cuts):
-            t = keep.tile([P, b - a, PACK], BF16, name=f"x_grp{i}", align_bytes=64)
-            for c in range(a, b, 256):
+        for i, (a, z) in enumerate(X_CUTS):
+            grouped = keep.tile([P, z - a, PACK], BF16, name=f"x_grouped{i}", align_bytes=64)
+            for c in range(a, z, 256):
                 part = slice(c - a, c - a + 256)
                 copy(
                     X_ENGINES[c // 256],
-                    t[:, part, :].rearrange("p (c i) j -> p c j i", i=4),
+                    grouped[:, part, :].rearrange("p (c i) j -> p c j i", i=4),
                     x_raw[i][:, :, part].rearrange("p j (c i) -> p c j i", i=4),
                 )
-            nc.vector.quantize_mx(out=xq[:, a:b].bitcast(FP8X4), scales=xs[:, a:b], in_=t[:].rearrange("p t j -> p (t j)"))
-        xq_slots, xs_slots = [], []
+            quantize(x_codes[:, a:z], x_scales[:, a:z], grouped)
+
+        slot_codes, slot_scales = {}, {}
 
         def gather(q):
-            o = slice(q * 2 * C // 16, (q + 1) * 2 * C // 16)
-            words = slot_pool.tile([P, 2 * C], U32, name="words", align_bytes=64)
-            scales = slot_pool.tile([P, 2 * C], U8, name="scales", align_bytes=64)
-            nc.vector.tensor_copy(words[:], xq[:].indirect(offs_t[:, o]))
-            nc.vector.tensor_copy(scales[:], xs[:].indirect(offs_t[:, o]))
-            xq_slots.append(words)
-            xs_slots.append(scales)
+            offsets = offs_t[:, q * PAIR // 16 : (q + 1) * PAIR // 16]
+            slot_codes[q] = slot_pool.tile([P, PAIR], U32, name="slot_codes", align_bytes=64)
+            slot_scales[q] = slot_pool.tile([P, PAIR], U8, name="slot_scales", align_bytes=64)
+            nc.vector.tensor_copy(slot_codes[q][:], x_codes[:].indirect(offsets))
+            nc.vector.tensor_copy(slot_scales[q][:], x_scales[:].indirect(offsets))
 
-        w1_codes, w1_scales, h_codes, h_scales = [], [], [], []
+        w1_codes, w1_scales = {}, {}
 
         def prepare_w1(e):
-            grp = w1g_pool.tile([P, H, PACK], BF16, name="w1_grp", align_bytes=64)
-            parts = W1_ENGINES[e]
-            size = P // len(parts)
-            for i in range(len(parts)):
+            grouped = grouped_pool.tile([P, H, PACK], BF16, name="w1_grouped", align_bytes=64)
+            engines = W1_ENGINES[e]
+            size = P // len(engines)
+            for i, engine in enumerate(engines):
                 m = slice(i * size, (i + 1) * size)
                 copy(
-                    parts[i],
-                    grp[:].rearrange("p (t m) j -> p m j t", t=PACK)[:, m, :, :],
+                    engine,
+                    grouped[:].rearrange("p (t m) j -> p m j t", t=PACK)[:, m, :, :],
                     w1_raw[e][:].rearrange("p j (m t) -> p m j t", t=PACK)[:, m, :, :],
                 )
-            codes = keep.tile([P, H], U32, name=f"w1_codes{e}", align_bytes=64)
-            scales = keep.tile([P, H], U8, name=f"w1_scales{e}", align_bytes=64)
-            nc.vector.quantize_mx(out=codes[:].bitcast(FP8X4), scales=scales[:], in_=grp[:].rearrange("p h j -> p (h j)"))
-            w1_codes.append(codes)
-            w1_scales.append(scales)
+            w1_codes[e] = codes_pool.tile([P, H], U32, name="w1_codes", align_bytes=64)
+            w1_scales[e] = codes_pool.tile([P, H], U8, name="w1_scales", align_bytes=64)
+            quantize(w1_codes[e][:], w1_scales[e][:], grouped)
 
-        h_grp = {}
-
-        def layer1(e):
-            if e % 2 == 0:
-                h_grp[e // 2] = h_pool.tile([P, 2 * C, PACK], BF16, name="h_grp", align_bytes=64)
-            grp = h_grp[e // 2]
-            base = e % 2 * C
-            for u in range(2):
+        def layer1(e, h_grouped):
+            for u in range(2 * (e % 2), 2 * (e % 2) + 2):
+                slots = slice(u * P, (u + 1) * P)
                 bank = psum_h.tile([P, PACK, P], F32, name="h_bank")
-                slots = slice(base + u * P, base + (u + 1) * P)
                 for t in range(PACK):
                     cols = slice(t * P, (t + 1) * P)
                     nc.tensor.matmul_mx(
                         out=bank[:, t, :],
                         lhsT=w1_codes[e][:, cols].bitcast(FP8X4),
                         lhsT_scale=w1_scales[e][:, cols],
-                        rhs=xq_slots[e // 2][:, slots].bitcast(FP8X4),
-                        rhs_scale=xs_slots[e // 2][:, slots],
+                        rhs=slot_codes[e // 2][:, slots].bitcast(FP8X4),
+                        rhs_scale=slot_scales[e // 2][:, slots],
                         start=True,
                         stop=True,
                     )
-                dst, src = grp[:, base + u * P : base + (u + 1) * P, :], bank[:].rearrange("p t s -> p s t")
-                if H_ENGINES[2 * e + u] == "S":
+                dst, src = h_grouped[:, slots, :], bank[:].rearrange("p t s -> p s t")
+                if H_ENGINES[e // 2 * 4 + u] == "S":
                     nc.scalar.activation(dst, src, RELU)
                 else:
                     nc.vector.tensor_relu(dst, src)
 
-        def quantize_h(q):
-            codes = keep.tile([P, 2 * C], U32, name=f"h_codes{q}", align_bytes=64)
-            scales = keep.tile([P, 2 * C], U8, name=f"h_scales{q}", align_bytes=64)
-            nc.vector.quantize_mx(out=codes[:].bitcast(FP8X4), scales=scales[:], in_=h_grp[q][:].rearrange("p s j -> p (s j)"))
-            h_codes.append(codes)
-            h_scales.append(scales)
+        h_codes, h_scales = {}, {}
+
+        def quantize_h(q, h_grouped):
+            h_codes[q] = keep.tile([P, PAIR], U32, name=f"h_codes{q}", align_bytes=64)
+            h_scales[q] = keep.tile([P, PAIR], U8, name=f"h_scales{q}", align_bytes=64)
+            quantize(h_codes[q][:], h_scales[q][:], h_grouped)
 
         w2_codes, w2_scales = {}, {}
 
-        def prepare_w2(half, q):
-            grp = h_pool.tile([P, 4 * P, PACK], BF16, name="w2_grp", align_bytes=64)
-            parts = W2_ENGINES[half][q]
-            size = 4 * P // len(parts)
-            for i in range(len(parts)):
-                n = slice(i * size, (i + 1) * size)
-                copy(
-                    parts[i],
-                    grp[:, n, :].rearrange("p (c i) j -> p c j i", i=4),
-                    w2_raw[half, q][:, :, n].rearrange("p j (c i) -> p c j i", i=4),
-                )
-            codes = w2_pool.tile([P, 4 * P], U32, name="w2_codes", align_bytes=64)
-            scales = w2_pool.tile([P, 4 * P], U8, name="w2_scales", align_bytes=64)
-            nc.vector.quantize_mx(out=codes[:].bitcast(FP8X4), scales=scales[:], in_=grp[:].rearrange("p n j -> p (n j)"))
-            w2_codes[half, q], w2_scales[half, q] = codes, scales
+        def prepare_w2(g):
+            experts, blocks = W2_GROUPS[g]
+            grouped = grouped_pool.tile([P, 4 * P, PACK], BF16, name="w2_grouped", align_bytes=64)
+            nc.vector.tensor_copy(
+                grouped[:].rearrange("p (c i) j -> p c j i", i=4), w2_raw[g][:].rearrange("p j (c i) -> p c j i", i=4)
+            )
+            codes = codes_pool.tile([P, 4 * P], U32, name="w2_codes", align_bytes=64)
+            scales = codes_pool.tile([P, 4 * P], U8, name="w2_scales", align_bytes=64)
+            quantize(codes[:], scales[:], grouped)
+            keys = [(e, b) for e in experts for b in blocks]
+            for i, key in enumerate(keys):
+                cols = slice(i * P, (i + 1) * P)
+                w2_codes[key], w2_scales[key] = codes[:, cols], scales[:, cols]
 
-        y_tiles = {}
+        y_tiles = [y_pool.tile([P, SLOTS], F32, name="y") for b in range(NB)]
 
         def layer2(b, q):
-            if q == 0:
-                y_tiles[b] = y_pool.tile([P, SLOTS], F32, name="y")
-            bank = psum_y.tile([P, 2 * C], F32, name="y_bank")
+            bank = psum_y.tile([P, PAIR], F32, name="y_bank")
             for r in range(2):
-                cols = slice((2 * r + b % 2) * P, (2 * r + b % 2 + 1) * P)
+                e = 2 * q + r
+                slots = slice(r * C, (r + 1) * C)
                 nc.tensor.matmul_mx(
-                    out=bank[:, r * C : (r + 1) * C],
-                    lhsT=w2_codes[b // 2, q][:, cols].bitcast(FP8X4),
-                    lhsT_scale=w2_scales[b // 2, q][:, cols],
-                    rhs=h_codes[q][:, r * C : (r + 1) * C].bitcast(FP8X4),
-                    rhs_scale=h_scales[q][:, r * C : (r + 1) * C],
+                    out=bank[:, slots],
+                    lhsT=w2_codes[e, b].bitcast(FP8X4),
+                    lhsT_scale=w2_scales[e, b],
+                    rhs=h_codes[q][:, slots].bitcast(FP8X4),
+                    rhs_scale=h_scales[q][:, slots],
                     start=True,
                     stop=True,
                 )
-            copy(Y_ENGINES[b * 3 + q], y_tiles[b][:, q * 2 * C : (q + 1) * 2 * C], bank[:])
+            nc.scalar.copy(y_tiles[b][:, q * PAIR : (q + 1) * PAIR], bank[:])
 
-        def combine(b):
-            first = work.tile([P, T], F32, name="first")
-            second = work.tile([P, T], F32, name="second")
-            cuts = ((0, 384), (384, 768)) if b == NB - 1 else ((0, T),)
-            y = y_tiles[b]
-            for a, z in cuts:
-                o = slice(a // 16, z // 16)
-                nc.vector.tensor_tensor(first[:, a:z], y[:].indirect(pos1_t[:, o]), gates[b, 0][:, a:z], MULT)
-                nc.vector.tensor_tensor(second[:, a:z], y[:].indirect(pos2_t[:, o]), gates[b, 1][:, a:z], MULT)
-                nc.vector.tensor_tensor(first[:, a:z], first[:, a:z], second[:, a:z], ADD)
-                nc.sync.dma_start(out=out[b * P : (b + 1) * P, a:z], in_=first[:, a:z])
+        whole = (slice(0, T),)
+        halves = (slice(0, T // 2), slice(T // 2, T))
 
-        gather(0)
-        prepare_w1(0)
-        prepare_w1(1)
-        layer1(0)
-        gather(1)
-        layer1(1)
-        prepare_w1(2)
-        quantize_h(0)
-        layer1(2)
-        prepare_w1(3)
-        gather(2)
-        layer1(3)
-        prepare_w1(4)
-        quantize_h(1)
-        layer1(4)
-        prepare_w1(5)
-        layer1(5)
-        load_w2(1)
-        prepare_w2(0, 0)
-        quantize_h(2)
-        layer2(0, 0)
-        prepare_w2(0, 1)
-        layer2(0, 1)
-        prepare_w2(0, 2)
+        def multiply(b, cuts):
+            products = [product_pool.tile([P, T], F32, name=f"product{r}") for r in range(2)]
+            for tokens in cuts:
+                part = slice(tokens.start // 16, tokens.stop // 16)
+                for r, offsets in enumerate((pos1_t, pos2_t)):
+                    nc.vector.tensor_tensor(
+                        products[r][:, tokens], y_tiles[b][:].indirect(offsets[:, part]), gates[b, r][:, tokens], MULT
+                    )
+            return products
+
+        def add_on_tensor(b, products):
+            for tokens in halves:
+                bank = psum_sum.tile([P, T // 2], F32, name="sum_bank")
+                for r in range(2):
+                    nc.tensor.matmul(bank[:], identity[:], products[r][:, tokens], start=(r == 0), stop=(r == 1))
+                result = result_pool.tile([P, T // 2], F32, name="result")
+                nc.scalar.copy(result[:], bank[:])
+                nc.sync.dma_start(out=out[b * P : (b + 1) * P, tokens], in_=result[:])
+
+        def add_on_vector(b, products):
+            for tokens in halves:
+                result = result_pool.tile([P, T // 2], F32, name="result")
+                nc.vector.tensor_tensor(result[:], products[0][:, tokens], products[1][:, tokens], ADD)
+                nc.sync.dma_start(out=out[b * P : (b + 1) * P, tokens], in_=result[:])
+
+        for q in range(E // 2):
+            gather(q)
+            h_grouped = grouped_pool.tile([P, PAIR, PACK], BF16, name="h_grouped", align_bytes=64)
+            for e in (2 * q, 2 * q + 1):
+                prepare_w1(e)
+                layer1(e, h_grouped)
+            quantize_h(q, h_grouped)
+            if q < 2:
+                for e in (2 * q, 2 * q + 1):
+                    prepare_w2(e)
+                for b in range(NB):
+                    layer2(b, q)
+            if q == 0:
+                load_w1(5)
+                load_w2(4)
+                load_gates(0)
+                load_w2(5)
+                for b in range(1, NB):
+                    load_gates(b)
+
+        prepare_w2(4)
         layer2(0, 2)
-        for q in range(E // 2):
-            layer2(1, q)
-        combine(0)
-        prepare_w2(1, 0)
-        layer2(2, 0)
-        prepare_w2(1, 1)
-        layer2(2, 1)
-        combine(1)
-        prepare_w2(1, 2)
+        layer2(1, 2)
+        products0 = multiply(0, whole)
+        prepare_w2(5)
         layer2(2, 2)
-        for q in range(E // 2):
-            layer2(3, q)
-        combine(2)
-        combine(3)
+        layer2(3, 2)
+        products1 = multiply(1, whole)
+        add_on_tensor(0, products0)
+        products2 = multiply(2, whole)
+        add_on_tensor(1, products1)
+        products3 = multiply(3, halves)
+        add_on_tensor(2, products2)
+        add_on_vector(3, products3)

@@ -23,9 +23,11 @@ NB = N // P
 PAIR = 2 * C
 
 X_CUTS = ((0, 512), (512, 768))
-X_ENGINES = "VSV"
-W1_ENGINES = ("S", "S", "S", "S", "VS", "VS")
-H_ENGINES = "SSSSSSVSVSVS"
+X_ENGINES = "VVS"
+W1_ENGINES = ("S", "S", "S", "V", "S", "V")
+W2_ENGINES = ("V", "S", "V", "VS", "V", "S")
+H_ENGINES = "SSSVSSVVSSVS"
+Y_ENGINES = "VSSSSSSSSSSS"
 ALL = tuple(range(NB))
 W2_GROUPS = (((0,), ALL), ((1,), ALL), ((2,), ALL), ((3,), ALL), ((4, 5), (0, 1)), ((4, 5), (2, 3)))
 
@@ -52,6 +54,7 @@ def tile_routed_moe_kernel(tc, xT, w1, w2, gate, offs, pos1, pos2, out):
         raw_pool = ctx.enter_context(tc.tile_pool(name="raw_pool", bufs=9))
         grouped_pool = ctx.enter_context(tc.tile_pool(name="grouped_pool", bufs=3))
         codes_pool = ctx.enter_context(tc.tile_pool(name="codes_pool", bufs=3))
+        w2_pool = ctx.enter_context(tc.tile_pool(name="w2_pool", bufs=4))
         slot_pool = ctx.enter_context(tc.tile_pool(name="slot_pool", bufs=2))
         y_pool = ctx.enter_context(tc.tile_pool(name="y_pool", bufs=NB))
         product_pool = ctx.enter_context(tc.tile_pool(name="product_pool", bufs=3))
@@ -94,16 +97,9 @@ def tile_routed_moe_kernel(tc, xT, w1, w2, gate, offs, pos1, pos2, out):
         nc.sync.dma_start(offs_t[:], offs)
         load_x(1)
         load_w1(0)
-        load_w1(1)
-        load_w2(0)
-        load_w2(1)
-        nc.sync.dma_start(pos1_t[:], pos1)
-        nc.sync.dma_start(pos2_t[:], pos2)
-        load_w1(2)
-        load_w1(3)
-        load_w2(2)
-        load_w2(3)
-        load_w1(4)
+        for e in range(1, 5):
+            load_w1(e)
+            load_w2(e - 1)
 
         identity = keep.tile([P, P], F32, name="identity")
         x_codes = keep.tile([P, T], U32, name="x_codes", align_bytes=64)
@@ -181,11 +177,17 @@ def tile_routed_moe_kernel(tc, xT, w1, w2, gate, offs, pos1, pos2, out):
         def prepare_w2(g):
             experts, blocks = W2_GROUPS[g]
             grouped = grouped_pool.tile([P, 4 * P, PACK], BF16, name="w2_grouped", align_bytes=64)
-            nc.vector.tensor_copy(
-                grouped[:].rearrange("p (c i) j -> p c j i", i=4), w2_raw[g][:].rearrange("p j (c i) -> p c j i", i=4)
-            )
-            codes = codes_pool.tile([P, 4 * P], U32, name="w2_codes", align_bytes=64)
-            scales = codes_pool.tile([P, 4 * P], U8, name="w2_scales", align_bytes=64)
+            engines = W2_ENGINES[g]
+            size = 4 * P // len(engines)
+            for i, engine in enumerate(engines):
+                cols = slice(i * size, (i + 1) * size)
+                copy(
+                    engine,
+                    grouped[:, cols, :].rearrange("p (c i) j -> p c j i", i=4),
+                    w2_raw[g][:, :, cols].rearrange("p j (c i) -> p c j i", i=4),
+                )
+            codes = w2_pool.tile([P, 4 * P], U32, name="w2_codes", align_bytes=64)
+            scales = w2_pool.tile([P, 4 * P], U8, name="w2_scales", align_bytes=64)
             quantize(codes[:], scales[:], grouped)
             keys = [(e, b) for e in experts for b in blocks]
             for i, key in enumerate(keys):
@@ -208,7 +210,7 @@ def tile_routed_moe_kernel(tc, xT, w1, w2, gate, offs, pos1, pos2, out):
                     start=True,
                     stop=True,
                 )
-            nc.scalar.copy(y_tiles[b][:, q * PAIR : (q + 1) * PAIR], bank[:])
+            copy(Y_ENGINES[3 * b + q], y_tiles[b][:, q * PAIR : (q + 1) * PAIR], bank[:])
 
         whole = (slice(0, T),)
         halves = (slice(0, T // 2), slice(T // 2, T))
@@ -253,9 +255,10 @@ def tile_routed_moe_kernel(tc, xT, w1, w2, gate, offs, pos1, pos2, out):
             if q == 0:
                 load_w1(5)
                 load_w2(4)
-                load_gates(0)
                 load_w2(5)
-                for b in range(1, NB):
+                nc.sync.dma_start(pos1_t[:], pos1)
+                nc.sync.dma_start(pos2_t[:], pos2)
+                for b in range(NB):
                     load_gates(b)
 
         prepare_w2(4)

from contextlib import ExitStack

import concourse.mybir as mybir
from concourse.masks import make_identity

K, T, E, C, H, N = 512, 768, 6, 256, 512, 512
SLOTS = E * C
FLOPS = 2 * SLOTS * (K * H + H * N)

F32 = mybir.dt.float32
BF16 = mybir.dt.bfloat16
U32 = mybir.dt.uint32
U16 = mybir.dt.uint16
U8 = mybir.dt.uint8
FP8X4 = mybir.dt.float8_e4m3fn_x4
MULT = mybir.AluOpType.mult
ADD = mybir.AluOpType.add
RELU = mybir.ActivationFunctionType.Relu

P = 128
PACK = 4
NB = N // P
PAIR = 2 * C

X_CUTS = ((0, 512), (512, 768))
X_ENGINES = "VVS"
W1_ENGINES = ("S", "S", "S", "V", "S", "V")
W2_ENGINES = ("V", "S", "V", "VS", "V", "S")
H_ENGINES = "SSSVSSVVSSVS"
Y_ENGINES = "VSSSSSSSSSSS"
ALL = tuple(range(NB))
W2_GROUPS = (((0,), ALL), ((1,), ALL), ((2,), ALL), ((3,), ALL), ((4, 5), (0, 1)), ((4, 5), (2, 3)))


def tile_routed_moe_kernel(tc, xT, w1, w2, gate, offs, pos1, pos2, out):
    nc = tc.nc

    def copy(engine, dst, src):
        if engine == "S":
            nc.scalar.copy(dst, src)
        else:
            nc.vector.tensor_copy(dst, src)

    def quantize(codes, scales, grouped):
        nc.vector.quantize_mx(out=codes.bitcast(FP8X4), scales=scales, in_=grouped[:].rearrange("p c j -> p (c j)"))

    with ExitStack() as ctx:
        lists = ctx.enter_context(tc.tile_pool(name="lists", bufs=1))
        offs_t = lists.tile([P, SLOTS // 16], U16, name="offs_t")
        pos1_t = lists.tile([P, T // 16], U16, name="pos1_t")
        pos2_t = lists.tile([P, T // 16], U16, name="pos2_t")

        keep = ctx.enter_context(tc.tile_pool(name="keep", bufs=1))
        raw_pool = ctx.enter_context(tc.tile_pool(name="raw_pool", bufs=9))
        grouped_pool = ctx.enter_context(tc.tile_pool(name="grouped_pool", bufs=3))
        codes_pool = ctx.enter_context(tc.tile_pool(name="codes_pool", bufs=3))
        w2_pool = ctx.enter_context(tc.tile_pool(name="w2_pool", bufs=4))
        slot_pool = ctx.enter_context(tc.tile_pool(name="slot_pool", bufs=2))
        y_pool = ctx.enter_context(tc.tile_pool(name="y_pool", bufs=NB))
        product_pool = ctx.enter_context(tc.tile_pool(name="product_pool", bufs=3))
        result_pool = ctx.enter_context(tc.tile_pool(name="result_pool", bufs=3))
        psum_h = ctx.enter_context(tc.psum_pool(name="psum_h", bufs=3))
        psum_y = ctx.enter_context(tc.psum_pool(name="psum_y", bufs=3))
        psum_sum = ctx.enter_context(tc.psum_pool(name="psum_sum", bufs=2))

        x_raw, w1_raw, w2_raw, gates = [], [], [], {}

        def load_x(i):
            a, z = X_CUTS[i]
            raw = keep.tile([P, PACK, z - a], F32, name=f"x_raw{i}")
            nc.sync.dma_start(out=raw[:], in_=xT.rearrange("(p j) t -> p j t", j=PACK)[:, :, a:z])
            x_raw.append(raw)

        def load_w1(e):
            raw = raw_pool.tile([P, PACK, H], F32, name="raw")
            nc.sync.dma_start(out=raw[:], in_=w1[e].rearrange("(p j) i -> p j i", j=PACK))
            w1_raw.append(raw)

        def load_w2(g):
            experts, blocks = W2_GROUPS[g]
            width = len(blocks) * P
            cols = slice(blocks[0] * P, blocks[0] * P + width)
            raw = raw_pool.tile([P, PACK, len(experts) * width], F32, name="raw")
            for r, e in enumerate(experts):
                nc.sync.dma_start(
                    out=raw[:, :, r * width : (r + 1) * width],
                    in_=w2[e].rearrange("(p j) n -> p j n", j=PACK)[:, :, cols],
                )
            w2_raw.append(raw)

        def load_gates(b):
            for r in range(2):
                gates[b, r] = keep.tile([P, T], F32, name=f"gate{b}_{r}")
                nc.sync.dma_start(out=gates[b, r][:], in_=gate[r, b * P : (b + 1) * P, :])

        load_x(0)
        nc.sync.dma_start(offs_t[:], offs)
        load_x(1)
        load_w1(0)
        for e in range(1, 5):
            load_w1(e)
            load_w2(e - 1)

        identity = keep.tile([P, P], F32, name="identity")
        x_codes = keep.tile([P, T], U32, name="x_codes", align_bytes=64)
        x_scales = keep.tile([P, T], U8, name="x_scales", align_bytes=64)
        nc.gpsimd.memset(x_scales[:], 0)
        make_identity(nc, identity[:])

        for i, (a, z) in enumerate(X_CUTS):
            grouped = keep.tile([P, z - a, PACK], BF16, name=f"x_grouped{i}", align_bytes=64)
            for c in range(a, z, 256):
                part = slice(c - a, c - a + 256)
                copy(
                    X_ENGINES[c // 256],
                    grouped[:, part, :].rearrange("p (c i) j -> p c j i", i=4),
                    x_raw[i][:, :, part].rearrange("p j (c i) -> p c j i", i=4),
                )
            quantize(x_codes[:, a:z], x_scales[:, a:z], grouped)

        slot_codes, slot_scales = {}, {}

        def gather(q):
            offsets = offs_t[:, q * PAIR // 16 : (q + 1) * PAIR // 16]
            slot_codes[q] = slot_pool.tile([P, PAIR], U32, name="slot_codes", align_bytes=64)
            slot_scales[q] = slot_pool.tile([P, PAIR], U8, name="slot_scales", align_bytes=64)
            nc.vector.tensor_copy(slot_codes[q][:], x_codes[:].indirect(offsets))
            nc.vector.tensor_copy(slot_scales[q][:], x_scales[:].indirect(offsets))

        w1_codes, w1_scales = {}, {}

        def prepare_w1(e):
            grouped = grouped_pool.tile([P, H, PACK], BF16, name="w1_grouped", align_bytes=64)
            engines = W1_ENGINES[e]
            size = P // len(engines)
            for i, engine in enumerate(engines):
                m = slice(i * size, (i + 1) * size)
                copy(
                    engine,
                    grouped[:].rearrange("p (t m) j -> p m j t", t=PACK)[:, m, :, :],
                    w1_raw[e][:].rearrange("p j (m t) -> p m j t", t=PACK)[:, m, :, :],
                )
            w1_codes[e] = codes_pool.tile([P, H], U32, name="w1_codes", align_bytes=64)
            w1_scales[e] = codes_pool.tile([P, H], U8, name="w1_scales", align_bytes=64)
            quantize(w1_codes[e][:], w1_scales[e][:], grouped)

        def layer1(e, h_grouped):
            for u in range(2 * (e % 2), 2 * (e % 2) + 2):
                slots = slice(u * P, (u + 1) * P)
                bank = psum_h.tile([P, PACK, P], F32, name="h_bank")
                for t in range(PACK):
                    cols = slice(t * P, (t + 1) * P)
                    nc.tensor.matmul_mx(
                        out=bank[:, t, :],
                        lhsT=w1_codes[e][:, cols].bitcast(FP8X4),
                        lhsT_scale=w1_scales[e][:, cols],
                        rhs=slot_codes[e // 2][:, slots].bitcast(FP8X4),
                        rhs_scale=slot_scales[e // 2][:, slots],
                        start=True,
                        stop=True,
                    )
                dst, src = h_grouped[:, slots, :], bank[:].rearrange("p t s -> p s t")
                if H_ENGINES[e // 2 * 4 + u] == "S":
                    nc.scalar.activation(dst, src, RELU)
                else:
                    nc.vector.tensor_relu(dst, src)

        h_codes, h_scales = {}, {}

        def quantize_h(q, h_grouped):
            h_codes[q] = keep.tile([P, PAIR], U32, name=f"h_codes{q}", align_bytes=64)
            h_scales[q] = keep.tile([P, PAIR], U8, name=f"h_scales{q}", align_bytes=64)
            quantize(h_codes[q][:], h_scales[q][:], h_grouped)

        w2_codes, w2_scales = {}, {}

        def prepare_w2(g):
            experts, blocks = W2_GROUPS[g]
            grouped = grouped_pool.tile([P, 4 * P, PACK], BF16, name="w2_grouped", align_bytes=64)
            engines = W2_ENGINES[g]
            size = 4 * P // len(engines)
            for i, engine in enumerate(engines):
                cols = slice(i * size, (i + 1) * size)
                copy(
                    engine,
                    grouped[:, cols, :].rearrange("p (c i) j -> p c j i", i=4),
                    w2_raw[g][:, :, cols].rearrange("p j (c i) -> p c j i", i=4),
                )
            codes = w2_pool.tile([P, 4 * P], U32, name="w2_codes", align_bytes=64)
            scales = w2_pool.tile([P, 4 * P], U8, name="w2_scales", align_bytes=64)
            quantize(codes[:], scales[:], grouped)
            keys = [(e, b) for e in experts for b in blocks]
            for i, key in enumerate(keys):
                cols = slice(i * P, (i + 1) * P)
                w2_codes[key], w2_scales[key] = codes[:, cols], scales[:, cols]

        y_tiles = [y_pool.tile([P, SLOTS], F32, name="y") for b in range(NB)]

        def layer2(b, q):
            bank = psum_y.tile([P, PAIR], F32, name="y_bank")
            for r in range(2):
                e = 2 * q + r
                slots = slice(r * C, (r + 1) * C)
                nc.tensor.matmul_mx(
                    out=bank[:, slots],
                    lhsT=w2_codes[e, b].bitcast(FP8X4),
                    lhsT_scale=w2_scales[e, b],
                    rhs=h_codes[q][:, slots].bitcast(FP8X4),
                    rhs_scale=h_scales[q][:, slots],
                    start=True,
                    stop=True,
                )
            copy(Y_ENGINES[3 * b + q], y_tiles[b][:, q * PAIR : (q + 1) * PAIR], bank[:])

        whole = (slice(0, T),)
        halves = (slice(0, T // 2), slice(T // 2, T))

        def multiply(b, cuts):
            products = [product_pool.tile([P, T], F32, name=f"product{r}") for r in range(2)]
            for tokens in cuts:
                part = slice(tokens.start // 16, tokens.stop // 16)
                for r, offsets in enumerate((pos1_t, pos2_t)):
                    nc.vector.tensor_tensor(
                        products[r][:, tokens], y_tiles[b][:].indirect(offsets[:, part]), gates[b, r][:, tokens], MULT
                    )
            return products

        def add_on_tensor(b, products):
            for tokens in halves:
                bank = psum_sum.tile([P, T // 2], F32, name="sum_bank")
                for r in range(2):
                    nc.tensor.matmul(bank[:], identity[:], products[r][:, tokens], start=(r == 0), stop=(r == 1))
                result = result_pool.tile([P, T // 2], F32, name="result")
                nc.scalar.copy(result[:], bank[:])
                nc.sync.dma_start(out=out[b * P : (b + 1) * P, tokens], in_=result[:])

        def add_on_vector(b, products):
            for tokens in halves:
                result = result_pool.tile([P, T // 2], F32, name="result")
                nc.vector.tensor_tensor(result[:], products[0][:, tokens], products[1][:, tokens], ADD)
                nc.sync.dma_start(out=out[b * P : (b + 1) * P, tokens], in_=result[:])

        for q in range(E // 2):
            gather(q)
            h_grouped = grouped_pool.tile([P, PAIR, PACK], BF16, name="h_grouped", align_bytes=64)
            for e in (2 * q, 2 * q + 1):
                prepare_w1(e)
                layer1(e, h_grouped)
            quantize_h(q, h_grouped)
            if q < 2:
                for e in (2 * q, 2 * q + 1):
                    prepare_w2(e)
                for b in range(NB):
                    layer2(b, q)
            if q == 0:
                load_w1(5)
                load_w2(4)
                load_w2(5)
                nc.sync.dma_start(pos1_t[:], pos1)
                nc.sync.dma_start(pos2_t[:], pos2)
                for b in range(NB):
                    load_gates(b)

        prepare_w2(4)
        layer2(0, 2)
        layer2(1, 2)
        products0 = multiply(0, whole)
        prepare_w2(5)
        layer2(2, 2)
        layer2(3, 2)
        products1 = multiply(1, whole)
        add_on_tensor(0, products0)
        products2 = multiply(2, whole)
        add_on_tensor(1, products1)
        products3 = multiply(3, halves)
        add_on_tensor(2, products2)
        add_on_vector(3, products3)
